import numpy as np
import ml_dtypes


def mxq(x, axis, fmt="e4m3"):
    dtype, down = {"e4m3": (ml_dtypes.float8_e4m3fn, 7), "e5m2": (ml_dtypes.float8_e5m2, 14)}[fmt]
    v = np.moveaxis(np.asarray(x, np.float32).astype(ml_dtypes.bfloat16).astype(np.float64), axis, -1)
    blocks = v.reshape(v.shape[:-1] + (-1, 32))
    amax = np.abs(blocks).max(-1, keepdims=True)
    byte = np.maximum(np.where(amax > 0, np.frexp(amax)[1] - 1 + 127, 0) - down, 1)
    scale = np.exp2(byte - 127.0)
    codes = (blocks / scale).astype(np.float32).astype(dtype).astype(np.float64)
    return np.moveaxis((codes * scale).reshape(v.shape), -1, axis)


WIDE = False


def mx_kscale(k):
    if not WIDE:
        return np.ones(k)
    levels = np.array([30, -30])
    if k % 512:
        return np.exp2(np.random.permutation(np.resize(levels, k // 32))).repeat(32)
    a = np.empty((k // 512, 16))
    for p in range(k // 512):
        a[p, :8] = np.random.permutation(np.resize(levels, 8))
        for g in range(8):
            far = levels[np.abs(levels - a[p, g]) >= 10]
            a[p, g + 8] = far[np.random.randint(len(far))]
    return np.exp2(a.ravel()).repeat(32)


def f64(x):
    return np.asarray(x).astype(np.float64)


def striped(idx):
    return np.tile(np.asarray(idx).reshape(-1, 16).T, (8, 1)).astype(np.uint16)


def unstriped(offs):
    return offs[:16].T.reshape(-1).astype(np.int64)


def striped8(idx):
    return np.asarray(idx).reshape(8, -1, 16).transpose(0, 2, 1).reshape(128, -1).astype(np.uint16)


def unstriped8(offs):
    return offs.reshape(8, 16, -1).transpose(0, 2, 1).reshape(8, -1).astype(np.int64)


def pick8(x, idx, run):
    r = np.arange(len(x))
    return x[r[:, None], idx[r % (8 * run) // run]]


E2M1 = np.array([0.0, 0.5, 1.0, 1.5, 2.0, 3.0, 4.0, 6.0, -0.0, -0.5, -1.0, -1.5, -2.0, -3.0, -4.0, -6.0])


def pack_weight(w, fmt):
    k, n = w.shape
    w = f64(np.asarray(w, np.float32).astype(ml_dtypes.bfloat16)).reshape(k // 32, 32, n)
    amax = np.abs(w).max(1)
    if fmt in ("e4m3", "e5m2"):
        byte = np.frexp(amax)[1] - 1 + 127 - (7 if fmt == "e4m3" else 14)
    else:
        mant, ex = np.frexp(amax / 6.0)
        byte = np.where(mant > 0.5, ex, ex - 1) + 127
    byte = np.clip(np.where(amax > 0, byte, 1), 1, 254)
    scaled = (w * np.exp2(127.0 - byte)[:, None, :]).reshape(k, n).astype(np.float32)
    by_word = np.ascontiguousarray(scaled.reshape(k // 512, 128, 4, n).transpose(0, 1, 3, 2))
    if fmt in ("e4m3", "e5m2"):
        words = by_word.astype(ml_dtypes.float8_e4m3fn if fmt == "e4m3" else ml_dtypes.float8_e5m2).view(np.uint8)
    else:
        c = by_word.astype(ml_dtypes.float4_e2m1fn).view(np.uint8) & 0xF
        words = (c[..., 0::2] | (c[..., 1::2] << 4)).reshape(k // 512, 128, 2 * n)
    return np.ascontiguousarray(words), np.ascontiguousarray(byte.astype(np.uint8).reshape(k // 512, 16, n))


def unpack_weight(words, scales, fmt):
    g, _, n = scales.shape
    words = np.ascontiguousarray(words).reshape(g, 128, n, -1)
    if fmt in ("e4m3", "e5m2"):
        vals = words.view(ml_dtypes.float8_e4m3fn if fmt == "e4m3" else ml_dtypes.float8_e5m2).astype(np.float64)
    else:
        nib = np.empty((g, 128, n, 4), np.uint8)
        nib[..., 0::2] = words & 0xF
        nib[..., 1::2] = words >> 4
        vals = E2M1[nib]
    vals = vals * np.repeat(np.exp2(scales.astype(np.float64) - 127.0), 8, axis=1)[..., None]
    return vals.transpose(0, 1, 3, 2).reshape(g * 512, n)


K, T, J, R, F, Z, C, O, N = 512, 1024, 256, 512, 512, 1024, 512, 128, 256


def setup_inputs():
    n = np.random.standard_normal
    idx = np.random.permutation(T)[:J]
    idx2 = np.random.permutation(Z)[:J]
    idx3 = np.stack([np.random.permutation(C)[:J] for _ in range(8)])
    idx4 = np.stack([np.random.permutation(C)[:J] for _ in range(8)])
    idx5 = np.random.permutation(C)[:O]
    idx6 = np.random.permutation(C)[:O]
    idx7 = np.random.permutation(T)[:O]
    fk = mx_kscale(K)
    ff = mx_kscale(F)
    fr = mx_kscale(R)
    xtp = pack_weight(n((K, T)) / fk[:, None], "e2m1")
    xop = pack_weight(n((F, Z)) / ff[:, None], "e5m2")
    wp = pack_weight(n((K, R)) * 1 / np.sqrt(K) * fk[:, None] * fr, "e5m2")
    w2p = pack_weight(n((F, R)) * 1 / np.sqrt(F) * ff[:, None] * fr, "e4m3")
    wbp = pack_weight(n((R, N)) * 1 / np.sqrt(R) / fr[:, None], "e4m3")
    wsp = pack_weight(n((K, N)) * 1 / np.sqrt(K) * fk[:, None], "e4m3")
    return {
        "xt_words": xtp[0],
        "xt_scales": xtp[1],
        "xo_words": xop[0],
        "xo_scales": xop[1],
        "w_words": wp[0],
        "w_scales": wp[1],
        "w2_words": w2p[0],
        "w2_scales": w2p[1],
        "sa": (np.random.uniform(0.5, 1.6, (R, 1))).astype(np.float32),
        "sb": (np.random.uniform(0.5, 1.6, (R, 1))).astype(np.float32),
        "wb_words": wbp[0],
        "wb_scales": wbp[1],
        "ws_words": wsp[0],
        "ws_scales": wsp[1],
        "offs": striped(idx),
        "offs2": striped(idx2),
        "offs3": striped8(idx3),
        "offs4": striped8(idx4),
        "offs5": striped(idx5),
        "offs6": striped(idx6),
        "offs7": striped(idx7),
    }


def reference(xt_words, xt_scales, xo_words, xo_scales, w_words, w_scales, w2_words, w2_scales, sa, sb, wb_words, wb_scales, ws_words, ws_scales, offs, offs2, offs3, offs4, offs5, offs6, offs7):
    idx = unstriped(offs)
    idx2 = unstriped(offs2)
    idx3 = unstriped8(offs3)
    idx4 = unstriped8(offs4)
    idx5 = unstriped(offs5)
    idx6 = unstriped(offs6)
    idx7 = unstriped(offs7)
    xtu = unpack_weight(xt_words, xt_scales, "e2m1")
    xou = unpack_weight(xo_words, xo_scales, "e5m2")
    wu = unpack_weight(w_words, w_scales, "e5m2")
    w2u = unpack_weight(w2_words, w2_scales, "e4m3")
    wbu = unpack_weight(wb_words, wb_scales, "e4m3")
    wsu = unpack_weight(ws_words, ws_scales, "e4m3")
    xtidxg = xtu[:, idx]
    a = wu.T @ xtidxg
    xoidx2g = xou[:, idx2]
    b = w2u.T @ xoidx2g
    pw = np.zeros((R, C))
    pw[np.arange(R)[:, None], idx3[np.arange(R) % 512 // 64]] = a
    pv = np.zeros((R, C))
    pv[np.arange(R)[:, None], idx4[np.arange(R) % 512 // 64]] = b
    pg = pw + pv
    hid = np.abs(pg[:, idx5] * f64(sa) - pg[:, idx6] * f64(sb))
    hidq = mxq(hid, 0, "e5m2")
    xtidx7g = xtu[:, idx7]
    y = wbu.T @ hidq + wsu.T @ xtidx7g
    return y

@@ -1,0 +1,218 @@
+from contextlib import ExitStack
+
+import concourse.mybir as mybir
+
+F32 = mybir.dt.float32
+BF16 = mybir.dt.bfloat16
+I32 = mybir.dt.int32
+U32 = mybir.dt.uint32
+U16 = mybir.dt.uint16
+U8 = mybir.dt.uint8
+E4M3 = mybir.dt.float8_e4m3fn_x4
+E5M2 = mybir.dt.float8_e5m2_x4
+E2M1 = mybir.dt.float4_e2m1fn_x4
+COPY = mybir.ActivationFunctionType.Copy
+ALU = mybir.AluOpType
+
+K, T, J, R, F, Z, C, O, N = 512, 1024, 256, 512, 512, 1024, 512, 128, 256
+P = 128
+PACK = 4
+QUADS = 4
+LANES = 16
+FLOPS = 2 * (K * R * J + F * R * J + R * N * O + K * N * O)
+
+
+def tile_list_ownsum_twotab_further_plain_kernel(
+    tc, xt_words, xt_scales, xo_words, xo_scales, w_words, w_scales, w2_words, w2_scales, sa, sb,
+    wb_words, wb_scales, ws_words, ws_scales, offs, offs2, offs3, offs4, offs5, offs6, offs7, out,
+):
+    nc = tc.nc
+    with ExitStack() as ctx:
+        lists = ctx.enter_context(tc.tile_pool(name="lists", bufs=1))
+        keep = ctx.enter_context(tc.tile_pool(name="keep", bufs=1))
+        ring = ctx.enter_context(tc.tile_pool(name="ring", bufs=2))
+        banks = ctx.enter_context(tc.psum_pool(name="banks", bufs=6))
+        y_banks = ctx.enter_context(tc.psum_pool(name="y_banks", bufs=1))
+
+        def load_list(source, name):
+            held = lists.tile(list(source.shape), U16, name=name)
+            nc.sync.dma_start(held[:], source)
+            return held
+
+        def entries(held, part):
+            return held[:, part.start // LANES : part.stop // LANES]
+
+        def load_words(queue, source, dtype, columns, name):
+            held = keep.tile([P, columns], dtype, name=name, tag=name, align_bytes=64)
+            queue.dma_start(held[:].bitcast(I32), source.bitcast(I32))
+            return held
+
+        def fp8_rows(words):
+            return words[0].rearrange("p n t -> p (n t)")
+
+        def zeroed_scales(columns, name):
+            held = keep.tile([P, columns], U8, name=name, align_bytes=64)
+            nc.vector.memset(held[:].bitcast(I32), 0)
+            return held
+
+        def load_scale_rows(queue, held, source, q):
+            queue.dma_start(held[32 * q : 32 * q + 4, :].bitcast(I32), source[0, 4 * q : 4 * q + 4, :].bitcast(I32))
+
+        def zeroed_board(name, tag):
+            held = keep.tile([P, C], F32, name=name, tag=tag, align_bytes=64)
+            nc.vector.memset(held[:], 0.0)
+            return held
+
+        def product(weights, weight_scales, weight_format, moving, moving_scales, moving_format, width):
+            bank = banks.tile([P, J], F32, name="bank")
+            nc.tensor.matmul_mx(
+                bank[:, 0:width], lhsT=weights.bitcast(weight_format), lhsT_scale=weight_scales,
+                rhs=moving.bitcast(moving_format), rhs_scale=moving_scales, start=True, stop=True,
+            )
+            return bank[:, 0:width]
+
+        xt_s = zeroed_scales(T, "xt_s")
+        w_s = zeroed_scales(R, "w_s")
+        idx = load_list(offs, "idx")
+        w_s_rows = keep.tile([PACK, QUADS, R // 4], I32, name="w_s_rows")
+        nc.sync.dma_start(w_s_rows[:], w_scales[0].bitcast(I32).rearrange("(q r) n -> r q n", r=4))
+        xt_w = load_words(nc.sync, xt_words[0], U16, T, "xt_w")
+        w_w = load_words(nc.sync, fp8_rows(w_words), U32, R, "w_w")
+        for q in range(QUADS):
+            load_scale_rows(nc.scalar, xt_s, xt_scales, q)
+        idx3 = load_list(offs3, "idx3")
+        pw = [zeroed_board("pw%d" % t, "pw%d" % t) for t in range(2)]
+
+        xo_s = zeroed_scales(Z, "xo_s")
+        w2_s = zeroed_scales(R, "w2_s")
+        ws_s = zeroed_scales(N, "ws_s")
+        wb_s = zeroed_scales(N, "wb_s")
+        idx2 = load_list(offs2, "idx2")
+        xo_w = load_words(nc.sync, fp8_rows(xo_words), U32, Z, "xo_w")
+        for q in range(QUADS):
+            load_scale_rows(nc.sync, xo_s, xo_scales, q)
+        w2_w = load_words(nc.sync, fp8_rows(w2_words), U32, R, "w2_w")
+        for q in range(QUADS):
+            load_scale_rows(nc.sync, w2_s, w2_scales, q)
+        idx4 = load_list(offs4, "idx4")
+        idx7 = load_list(offs7, "idx7")
+        idx5 = load_list(offs5, "idx5")
+        idx6 = load_list(offs6, "idx6")
+        sa_t = keep.tile([P, PACK], F32, name="sa_t")
+        nc.sync.dma_start(sa_t[:], sa.rearrange("(p t) o -> p (t o)", t=PACK))
+        sb_t = keep.tile([P, PACK], F32, name="sb_t")
+        nc.sync.dma_start(sb_t[:], sb.rearrange("(p t) o -> p (t o)", t=PACK))
+        ws_w = load_words(nc.sync, fp8_rows(ws_words), U32, N, "ws_w")
+        for q in range(QUADS):
+            load_scale_rows(nc.sync, ws_s, ws_scales, q)
+        wb_w = load_words(nc.sync, fp8_rows(wb_words), U32, N, "wb_w")
+        for q in range(QUADS):
+            load_scale_rows(nc.sync, wb_s, wb_scales, q)
+
+        for q in range(QUADS):
+            nc.vector.tensor_copy(w_s[32 * q : 32 * q + 4, :].bitcast(I32), w_s_rows[:, q, :])
+        w_ts = keep.tile([P, PACK, P], U8, name="w_ts", align_bytes=64)
+        nc.vector.tensor_copy(w_ts[:], w_s[:].rearrange("p (m t) -> p t m", t=PACK))
+        w_first = keep.tile([P, P], U32, name="w_first", align_bytes=64)
+        w_rest = keep.tile([P, PACK - 1, P], U32, name="w_rest", align_bytes=64)
+        nc.scalar.copy(w_first[:], w_w[:, 0:R:PACK])
+        nc.scalar.copy(w_rest[:].rearrange("p t m -> p m t"), w_w[:].rearrange("p (m t) -> p m t", t=PACK)[:, :, 1:PACK])
+        w_t = [w_first[:]] + [w_rest[:, t, :] for t in range(PACK - 1)]
+        xg_w = keep.tile([P, J], U16, name="xg_w", align_bytes=64)
+        xg_s = keep.tile([P, J], U8, name="xg_s", align_bytes=64)
+        a_sb = [keep.tile([P, J], F32, name="a_sb%d" % t) for t in range(PACK)]
+
+        def put_a(t, part, leave_bank):
+            bank = product(w_t[t], w_ts[:, t, :], E5M2, xg_w[:, part], xg_s[:, part], E2M1, part.stop - part.start)
+            leave_bank(a_sb[t][:, part], bank)
+            nc.scalar.activation(pw[t][:].indirect(entries(idx3, part)), a_sb[t][:, part], COPY)
+
+        for h in range(2):
+            part = slice(h * J // 2, (h + 1) * J // 2)
+            nc.vector.tensor_copy(xg_w[:, part], xt_w[:].indirect(entries(idx, part)))
+            nc.vector.tensor_copy(xg_s[:, part], xt_s[:].indirect(entries(idx, part)))
+            put_a(0, part, nc.scalar.copy if h == 0 else nc.vector.tensor_copy)
+            put_a(1, part, nc.vector.tensor_copy)
+        pw.append(zeroed_board("pw2", "w_w"))
+        pw.append(pw[0])
+        put_a(2, slice(0, J), nc.vector.tensor_copy)
+        bank = product(w_t[3], w_ts[:, 3, :], E5M2, xg_w[:], xg_s[:], E2M1, J)
+        nc.vector.tensor_copy(a_sb[3][:], bank)
+
+        og_w = keep.tile([P, J], U32, name="og_w", align_bytes=64)
+        og_s = keep.tile([P, J], U8, name="og_s", align_bytes=64)
+        nc.vector.tensor_copy(og_w[:], xo_w[:].indirect(idx2[:]))
+        nc.vector.tensor_copy(og_s[:], xo_s[:].indirect(idx2[:]))
+        w2_t = keep.tile([P, PACK, P], U32, name="w2_t", align_bytes=64)
+        w2_ts = keep.tile([P, PACK, P], U8, name="w2_ts", align_bytes=64)
+        nc.vector.tensor_copy(
+            w2_t[:].bitcast(I32).rearrange("p t m -> p m t"), w2_w[:].bitcast(I32).rearrange("p (m t) -> p m t", t=PACK)
+        )
+        nc.vector.tensor_copy(w2_ts[:], w2_s[:].rearrange("p (m t) -> p t m", t=PACK))
+        pv = [zeroed_board("pv0", "xo_w"), zeroed_board("pv1", "w2_w")]
+        b_sb = [keep.tile([P, J], F32, name="b_sb%d" % t) for t in range(PACK)]
+        for t in range(PACK):
+            bank = product(w2_t[:, t, :], w2_ts[:, t, :], E4M3, og_w[:], og_s[:], E5M2, J)
+            nc.vector.tensor_copy(b_sb[t][:], bank)
+
+        x7_w = keep.tile([P, O], U16, name="x7_w", align_bytes=64)
+        x7_s = keep.tile([P, O], U8, name="x7_s", align_bytes=64)
+        nc.vector.tensor_copy(x7_w[:], xt_w[:].indirect(idx7[:]))
+        nc.vector.tensor_copy(x7_s[:], xt_s[:].indirect(idx7[:]))
+        y = [y_banks.tile([P, O], F32, name="y%d" % u) for u in range(N // P)]
+        for u in range(N // P):
+            cols = slice(u * P, (u + 1) * P)
+            nc.tensor.matmul_mx(
+                y[u][:], lhsT=ws_w[:, cols].bitcast(E4M3), lhsT_scale=ws_s[:, cols],
+                rhs=x7_w[:].bitcast(E2M1), rhs_scale=x7_s[:], start=True, stop=False,
+            )
+
+        diff = [keep.tile([P, PACK, O // 2], F32, name="diff%d" % h) for h in range(2)]
+        hid = [keep.tile([P, O // 2, PACK], BF16, name="hid%d" % h, align_bytes=64) for h in range(2)]
+        hid_w = keep.tile([P, O], U32, name="hid_w", align_bytes=64)
+        hid_s = keep.tile([P, O], U8, name="hid_s", align_bytes=64)
+        halves = [slice(0, O // 2), slice(O // 2, O)]
+        boards = {}
+
+        def put_b(t):
+            nc.scalar.activation(pv[t % 2][:].indirect(idx4[:]), b_sb[t][:], COPY)
+            pg = ring.tile([P, C], F32, name="pg")
+            nc.vector.tensor_tensor(pg[:], pw[t][:], pv[t % 2][:], ALU.add)
+            boards[t] = pg
+
+        def pick(t, parts):
+            first = ring.tile([P, O], F32, name="first")
+            second = ring.tile([P, O], F32, name="second")
+            for part in parts:
+                nc.scalar.activation(first[:, part], boards[t][:].indirect(entries(idx5, part)), COPY, scale=sa_t[:, t : t + 1])
+                nc.scalar.activation(second[:, part], boards[t][:].indirect(entries(idx6, part)), COPY, scale=sb_t[:, t : t + 1])
+            for h in range(2):
+                nc.vector.tensor_tensor(diff[h][:, t, :], first[:, halves[h]], second[:, halves[h]], ALU.subtract)
+            if t % 2 == 1:
+                for h in range(2):
+                    pair = diff[h][:, t - 1 : t + 1, :].rearrange("p t o -> p o t")
+                    nc.vector.scalar_tensor_tensor(hid[h][:, :, t - 1 : t + 1], pair, -1.0, pair, ALU.mult, ALU.max)
+
+        put_b(0)
+        for t in range(1, PACK):
+            put_b(t)
+            pick(t - 1, [slice(0, O)])
+            if t == 1:
+                nc.scalar.activation(pw[3][:].indirect(idx3[:]), a_sb[3][:], COPY)
+        pick(PACK - 1, halves)
+
+        for h in range(2):
+            nc.vector.quantize_mx(hid_w[:, halves[h]].bitcast(E5M2), hid_s[:, halves[h]], hid[h][:].rearrange("p o t -> p (o t)"))
+        for u in range(N // P):
+            cols = slice(u * P, (u + 1) * P)
+            nc.tensor.matmul_mx(
+                y[u][:], lhsT=wb_w[:, cols].bitcast(E4M3), lhsT_scale=wb_s[:, cols],
+                rhs=hid_w[:].bitcast(E5M2), rhs_scale=hid_s[:], start=False, stop=True,
+            )
+            y_sb = keep.tile([P, O], F32, name="y_sb%d" % u)
+            if u == 0:
+                nc.vector.tensor_copy(y_sb[:], y[u][:])
+                nc.sync.dma_start(out[cols, :], y_sb[:])
+            else:
+                nc.scalar.copy(y_sb[:], y[u][:])
+                nc.scalar.dma_start(out[cols, :], y_sb[:])

@@ -31,8 +31,7 @@ def tile_list_ownsum_twotab_further_plain_kernel(
         lists = ctx.enter_context(tc.tile_pool(name="lists", bufs=1))
         keep = ctx.enter_context(tc.tile_pool(name="keep", bufs=1))
         ring = ctx.enter_context(tc.tile_pool(name="ring", bufs=2))
-        banks = ctx.enter_context(tc.psum_pool(name="banks", bufs=6))
-        y_banks = ctx.enter_context(tc.psum_pool(name="y_banks", bufs=1))
+        banks = ctx.enter_context(tc.psum_pool(name="banks", bufs=1))
 
         def load_list(source, name):
             held = lists.tile(list(source.shape), U16, name=name)
@@ -42,8 +41,8 @@ def tile_list_ownsum_twotab_further_plain_kernel(
         def entries(held, part):
             return held[:, part.start // LANES : part.stop // LANES]
 
-        def load_words(queue, source, dtype, columns, name):
-            held = keep.tile([P, columns], dtype, name=name, tag=name, align_bytes=64)
+        def load_words(queue, source, dtype, columns, name, tag):
+            held = keep.tile([P, columns], dtype, name=name, tag=tag, align_bytes=64)
             queue.dma_start(held[:].bitcast(I32), source.bitcast(I32))
             return held
 
@@ -51,20 +50,20 @@ def tile_list_ownsum_twotab_further_plain_kernel(
             return words[0].rearrange("p n t -> p (n t)")
 
         def zeroed_scales(columns, name):
-            held = keep.tile([P, columns], U8, name=name, align_bytes=64)
+            held = keep.tile([P, columns], U8, name=name, tag=name, align_bytes=64)
             nc.vector.memset(held[:].bitcast(I32), 0)
             return held
 
         def load_scale_rows(queue, held, source, q):
             queue.dma_start(held[32 * q : 32 * q + 4, :].bitcast(I32), source[0, 4 * q : 4 * q + 4, :].bitcast(I32))
 
-        def zeroed_board(name, tag):
+        def zeroed_board(engine, name, tag):
             held = keep.tile([P, C], F32, name=name, tag=tag, align_bytes=64)
-            nc.vector.memset(held[:], 0.0)
+            engine.memset(held[:], 0.0)
             return held
 
-        def product(weights, weight_scales, weight_format, moving, moving_scales, moving_format, width):
-            bank = banks.tile([P, J], F32, name="bank")
+        def product(weights, weight_scales, weight_format, moving, moving_scales, moving_format, width, place):
+            bank = banks.tile([P, J], F32, name="bank", tag="bank%d" % place)
             nc.tensor.matmul_mx(
                 bank[:, 0:width], lhsT=weights.bitcast(weight_format), lhsT_scale=weight_scales,
                 rhs=moving.bitcast(moving_format), rhs_scale=moving_scales, start=True, stop=True,
@@ -73,57 +72,51 @@ def tile_list_ownsum_twotab_further_plain_kernel(
 
         xt_s = zeroed_scales(T, "xt_s")
         w_s = zeroed_scales(R, "w_s")
+        xo_s = zeroed_scales(Z, "xo_s")
+        w2_s = zeroed_scales(R, "w2_s")
         idx = load_list(offs, "idx")
-        w_s_rows = keep.tile([PACK, QUADS, R // 4], I32, name="w_s_rows")
+        w_s_rows = keep.tile([PACK, QUADS, R // 4], I32, name="w_s_rows", tag="w_s_rows", align_bytes=64)
         nc.sync.dma_start(w_s_rows[:], w_scales[0].bitcast(I32).rearrange("(q r) n -> r q n", r=4))
-        xt_w = load_words(nc.sync, xt_words[0], U16, T, "xt_w")
-        w_w = load_words(nc.sync, fp8_rows(w_words), U32, R, "w_w")
+        xt_w = load_words(nc.sync, xt_words[0], U16, T, "xt_w", "xt_w")
+        w_w = load_words(nc.sync, fp8_rows(w_words), U32, R, "w_w", "w_w")
         for q in range(QUADS):
             load_scale_rows(nc.scalar, xt_s, xt_scales, q)
         idx3 = load_list(offs3, "idx3")
-        pw = [zeroed_board("pw%d" % t, "pw%d" % t) for t in range(2)]
+        pw = [zeroed_board(nc.vector, "pw%d" % t, "pw%d" % t) for t in range(2)]
 
-        xo_s = zeroed_scales(Z, "xo_s")
-        w2_s = zeroed_scales(R, "w2_s")
         ws_s = zeroed_scales(N, "ws_s")
         wb_s = zeroed_scales(N, "wb_s")
         idx2 = load_list(offs2, "idx2")
-        xo_w = load_words(nc.sync, fp8_rows(xo_words), U32, Z, "xo_w")
         for q in range(QUADS):
             load_scale_rows(nc.sync, xo_s, xo_scales, q)
-        w2_w = load_words(nc.sync, fp8_rows(w2_words), U32, R, "w2_w")
+        xo_w = load_words(nc.sync, fp8_rows(xo_words), U32, Z, "xo_w", "xo_w")
+        w2_w = load_words(nc.sync, fp8_rows(w2_words), U32, R, "w2_w", "w2_w")
         for q in range(QUADS):
             load_scale_rows(nc.sync, w2_s, w2_scales, q)
         idx4 = load_list(offs4, "idx4")
         idx7 = load_list(offs7, "idx7")
         idx5 = load_list(offs5, "idx5")
         idx6 = load_list(offs6, "idx6")
-        sa_t = keep.tile([P, PACK], F32, name="sa_t")
-        nc.sync.dma_start(sa_t[:], sa.rearrange("(p t) o -> p (t o)", t=PACK))
-        sb_t = keep.tile([P, PACK], F32, name="sb_t")
-        nc.sync.dma_start(sb_t[:], sb.rearrange("(p t) o -> p (t o)", t=PACK))
-        ws_w = load_words(nc.sync, fp8_rows(ws_words), U32, N, "ws_w")
         for q in range(QUADS):
             load_scale_rows(nc.sync, ws_s, ws_scales, q)
-        wb_w = load_words(nc.sync, fp8_rows(wb_words), U32, N, "wb_w")
         for q in range(QUADS):
             load_scale_rows(nc.sync, wb_s, wb_scales, q)
 
         for q in range(QUADS):
             nc.vector.tensor_copy(w_s[32 * q : 32 * q + 4, :].bitcast(I32), w_s_rows[:, q, :])
-        w_ts = keep.tile([P, PACK, P], U8, name="w_ts", align_bytes=64)
+        w_ts = keep.tile([P, PACK, P], U8, name="w_ts", tag="w_ts", align_bytes=64)
         nc.vector.tensor_copy(w_ts[:], w_s[:].rearrange("p (m t) -> p t m", t=PACK))
-        w_first = keep.tile([P, P], U32, name="w_first", align_bytes=64)
+        w_first = keep.tile([P, P], U32, name="w_first", tag="w_first", align_bytes=64)
         w_rest = keep.tile([P, PACK - 1, P], U32, name="w_rest", align_bytes=64)
         nc.scalar.copy(w_first[:], w_w[:, 0:R:PACK])
         nc.scalar.copy(w_rest[:].rearrange("p t m -> p m t"), w_w[:].rearrange("p (m t) -> p m t", t=PACK)[:, :, 1:PACK])
         w_t = [w_first[:]] + [w_rest[:, t, :] for t in range(PACK - 1)]
         xg_w = keep.tile([P, J], U16, name="xg_w", align_bytes=64)
         xg_s = keep.tile([P, J], U8, name="xg_s", align_bytes=64)
-        a_sb = [keep.tile([P, J], F32, name="a_sb%d" % t) for t in range(PACK)]
+        a_sb = [keep.tile([P, J], F32, name="a_sb%d" % t, tag="a_sb%d" % t, align_bytes=64) for t in range(PACK)]
 
-        def put_a(t, part, leave_bank):
-            bank = product(w_t[t], w_ts[:, t, :], E5M2, xg_w[:, part], xg_s[:, part], E2M1, part.stop - part.start)
+        def put_a(t, part, leave_bank, place):
+            bank = product(w_t[t], w_ts[:, t, :], E5M2, xg_w[:, part], xg_s[:, part], E2M1, part.stop - part.start, place)
             leave_bank(a_sb[t][:, part], bank)
             nc.scalar.activation(pw[t][:].indirect(entries(idx3, part)), a_sb[t][:, part], COPY)
 
@@ -131,13 +124,19 @@ def tile_list_ownsum_twotab_further_plain_kernel(
             part = slice(h * J // 2, (h + 1) * J // 2)
             nc.vector.tensor_copy(xg_w[:, part], xt_w[:].indirect(entries(idx, part)))
             nc.vector.tensor_copy(xg_s[:, part], xt_s[:].indirect(entries(idx, part)))
-            put_a(0, part, nc.scalar.copy if h == 0 else nc.vector.tensor_copy)
-            put_a(1, part, nc.vector.tensor_copy)
-        pw.append(zeroed_board("pw2", "w_w"))
-        pw.append(pw[0])
-        put_a(2, slice(0, J), nc.vector.tensor_copy)
-        bank = product(w_t[3], w_ts[:, 3, :], E5M2, xg_w[:], xg_s[:], E2M1, J)
+            put_a(0, part, nc.scalar.copy if h == 0 else nc.vector.tensor_copy, 2 * h)
+            put_a(1, part, nc.vector.tensor_copy, 2 * h + 1)
+        pw.append(zeroed_board(nc.gpsimd, "pw2", "w_w"))
+        put_a(2, slice(0, J), nc.vector.tensor_copy, 4)
+        bank = product(w_t[3], w_ts[:, 3, :], E5M2, xg_w[:], xg_s[:], E2M1, J, 5)
         nc.vector.tensor_copy(a_sb[3][:], bank)
+
+        ws_w = load_words(nc.sync, fp8_rows(ws_words), U32, N, "ws_w", "w_s_rows")
+        wb_w = load_words(nc.sync, fp8_rows(wb_words), U32, N, "wb_w", "w_s")
+        sa_t = keep.tile([P, PACK], F32, name="sa_t", tag="w_first", align_bytes=64)
+        nc.sync.dma_start(sa_t[:], sa.rearrange("(p t) o -> p (t o)", t=PACK))
+        sb_t = keep.tile([P, PACK], F32, name="sb_t", tag="w_ts", align_bytes=64)
+        nc.sync.dma_start(sb_t[:], sb.rearrange("(p t) o -> p (t o)", t=PACK))
 
         og_w = keep.tile([P, J], U32, name="og_w", align_bytes=64)
         og_s = keep.tile([P, J], U8, name="og_s", align_bytes=64)
@@ -149,17 +148,21 @@ def tile_list_ownsum_twotab_further_plain_kernel(
             w2_t[:].bitcast(I32).rearrange("p t m -> p m t"), w2_w[:].bitcast(I32).rearrange("p (m t) -> p m t", t=PACK)
         )
         nc.vector.tensor_copy(w2_ts[:], w2_s[:].rearrange("p (m t) -> p t m", t=PACK))
-        pv = [zeroed_board("pv0", "xo_w"), zeroed_board("pv1", "w2_w")]
+        pw.append(zeroed_board(nc.gpsimd, "pw3", "xo_w"))
+        nc.scalar.activation(pw[3][:].indirect(idx3[:]), a_sb[3][:], COPY)
+        pv = []
         b_sb = [keep.tile([P, J], F32, name="b_sb%d" % t) for t in range(PACK)]
         for t in range(PACK):
-            bank = product(w2_t[:, t, :], w2_ts[:, t, :], E4M3, og_w[:], og_s[:], E5M2, J)
+            bank = product(w2_t[:, t, :], w2_ts[:, t, :], E4M3, og_w[:], og_s[:], E5M2, J, t)
             nc.vector.tensor_copy(b_sb[t][:], bank)
+            if t < 2:
+                pv.append(zeroed_board(nc.gpsimd, "pv%d" % t, ("w2_w", "a_sb0")[t]))
 
         x7_w = keep.tile([P, O], U16, name="x7_w", align_bytes=64)
         x7_s = keep.tile([P, O], U8, name="x7_s", align_bytes=64)
         nc.vector.tensor_copy(x7_w[:], xt_w[:].indirect(idx7[:]))
         nc.vector.tensor_copy(x7_s[:], xt_s[:].indirect(idx7[:]))
-        y = [y_banks.tile([P, O], F32, name="y%d" % u) for u in range(N // P)]
+        y = [banks.tile([P, O], F32, name="y%d" % u, tag="bank%d" % (2 + u)) for u in range(N // P)]
         for u in range(N // P):
             cols = slice(u * P, (u + 1) * P)
             nc.tensor.matmul_mx(
@@ -197,8 +200,6 @@ def tile_list_ownsum_twotab_further_plain_kernel(
         for t in range(1, PACK):
             put_b(t)
             pick(t - 1, [slice(0, O)])
-            if t == 1:
-                nc.scalar.activation(pw[3][:].indirect(idx3[:]), a_sb[3][:], COPY)
         pick(PACK - 1, halves)
 
         for h in range(2):

@@ -17,8 +17,11 @@ ALU = mybir.AluOpType
 K, T, J, R, F, Z, C, O, N = 512, 1024, 256, 512, 512, 1024, 512, 128, 256
 P = 128
 PACK = 4
-QUADS = 4
-LANES = 16
+QUADRANTS = 4
+QUADRANT = P // QUADRANTS
+SCALE_ROWS = 4
+LIST_ROWS = 16
+MX_ALIGN = 64
 FLOPS = 2 * (K * R * J + F * R * J + R * N * O + K * N * O)
 
 
@@ -39,26 +42,36 @@ def tile_list_ownsum_twotab_further_plain_kernel(
             return held
 
         def entries(held, part):
-            return held[:, part.start // LANES : part.stop // LANES]
+            return held[:, part.start // LIST_ROWS : part.stop // LIST_ROWS]
 
-        def load_words(queue, source, dtype, columns, name, tag):
-            held = keep.tile([P, columns], dtype, name=name, tag=tag, align_bytes=64)
-            queue.dma_start(held[:].bitcast(I32), source.bitcast(I32))
+        def load_words(source, dtype, columns, name):
+            held = keep.tile([P, columns], dtype, name=name, tag=name, align_bytes=MX_ALIGN)
+            nc.sync.dma_start(held[:].bitcast(I32), source.bitcast(I32))
             return held
 
         def fp8_rows(words):
             return words[0].rearrange("p n t -> p (n t)")
 
         def zeroed_scales(columns, name):
-            held = keep.tile([P, columns], U8, name=name, tag=name, align_bytes=64)
+            held = keep.tile([P, columns], U8, name=name, align_bytes=MX_ALIGN)
             nc.vector.memset(held[:].bitcast(I32), 0)
             return held
 
-        def load_scale_rows(queue, held, source, q):
-            queue.dma_start(held[32 * q : 32 * q + 4, :].bitcast(I32), source[0, 4 * q : 4 * q + 4, :].bitcast(I32))
+        def live_rows(held, q):
+            return held[QUADRANT * q : QUADRANT * q + SCALE_ROWS, :].bitcast(I32)
+
+        def load_scales(held, source):
+            for q in range(QUADRANTS):
+                rows = source[0, SCALE_ROWS * q : SCALE_ROWS * (q + 1), :]
+                nc.sync.dma_start(live_rows(held, q), rows.bitcast(I32))
+
+        def load_row_weights(source, name):
+            held = keep.tile([P, PACK], F32, name=name)
+            nc.sync.dma_start(held[:], source.rearrange("(p t) o -> p (t o)", t=PACK))
+            return held
 
         def zeroed_board(engine, name, tag):
-            held = keep.tile([P, C], F32, name=name, tag=tag, align_bytes=64)
+            held = keep.tile([P, C], F32, name=name, tag=tag, align_bytes=MX_ALIGN)
             engine.memset(held[:], 0.0)
             return held
 
@@ -75,91 +88,91 @@ def tile_list_ownsum_twotab_further_plain_kernel(
         xo_s = zeroed_scales(Z, "xo_s")
         w2_s = zeroed_scales(R, "w2_s")
         idx = load_list(offs, "idx")
-        w_s_rows = keep.tile([PACK, QUADS, R // 4], I32, name="w_s_rows", tag="w_s_rows", align_bytes=64)
-        nc.sync.dma_start(w_s_rows[:], w_scales[0].bitcast(I32).rearrange("(q r) n -> r q n", r=4))
-        xt_w = load_words(nc.sync, xt_words[0], U16, T, "xt_w", "xt_w")
-        w_w = load_words(nc.sync, fp8_rows(w_words), U32, R, "w_w", "w_w")
-        for q in range(QUADS):
-            load_scale_rows(nc.scalar, xt_s, xt_scales, q)
+        w_s_rows = keep.tile([SCALE_ROWS, QUADRANTS, R // 4], I32, name="w_s_rows")
+        nc.sync.dma_start(w_s_rows[:], w_scales[0].bitcast(I32).rearrange("(q i) n -> i q n", i=SCALE_ROWS))
+        xt_w = load_words(xt_words[0], U16, T, "xt_w")
+        load_scales(xt_s, xt_scales)
+        w_w = load_words(fp8_rows(w_words), U32, R, "w_w")
         idx3 = load_list(offs3, "idx3")
         pw = [zeroed_board(nc.vector, "pw%d" % t, "pw%d" % t) for t in range(2)]
 
         ws_s = zeroed_scales(N, "ws_s")
         wb_s = zeroed_scales(N, "wb_s")
         idx2 = load_list(offs2, "idx2")
-        for q in range(QUADS):
-            load_scale_rows(nc.sync, xo_s, xo_scales, q)
-        xo_w = load_words(nc.sync, fp8_rows(xo_words), U32, Z, "xo_w", "xo_w")
-        w2_w = load_words(nc.sync, fp8_rows(w2_words), U32, R, "w2_w", "w2_w")
-        for q in range(QUADS):
-            load_scale_rows(nc.sync, w2_s, w2_scales, q)
+        load_scales(xo_s, xo_scales)
+        xo_w = load_words(fp8_rows(xo_words), U32, Z, "xo_w")
+        w2_w = load_words(fp8_rows(w2_words), U32, R, "w2_w")
+        load_scales(w2_s, w2_scales)
         idx4 = load_list(offs4, "idx4")
         idx7 = load_list(offs7, "idx7")
         idx5 = load_list(offs5, "idx5")
         idx6 = load_list(offs6, "idx6")
-        for q in range(QUADS):
-            load_scale_rows(nc.sync, ws_s, ws_scales, q)
-        for q in range(QUADS):
-            load_scale_rows(nc.sync, wb_s, wb_scales, q)
+        sa_t = load_row_weights(sa, "sa_t")
+        sb_t = load_row_weights(sb, "sb_t")
+        ws_w = load_words(fp8_rows(ws_words), U32, N, "ws_w")
+        load_scales(ws_s, ws_scales)
+        wb_w = load_words(fp8_rows(wb_words), U32, N, "wb_w")
+        load_scales(wb_s, wb_scales)
 
-        for q in range(QUADS):
-            nc.vector.tensor_copy(w_s[32 * q : 32 * q + 4, :].bitcast(I32), w_s_rows[:, q, :])
-        w_ts = keep.tile([P, PACK, P], U8, name="w_ts", tag="w_ts", align_bytes=64)
-        nc.vector.tensor_copy(w_ts[:], w_s[:].rearrange("p (m t) -> p t m", t=PACK))
-        w_first = keep.tile([P, P], U32, name="w_first", tag="w_first", align_bytes=64)
-        w_rest = keep.tile([P, PACK - 1, P], U32, name="w_rest", align_bytes=64)
+        for q in range(QUADRANTS):
+            nc.vector.tensor_copy(live_rows(w_s, q), w_s_rows[:, q, :])
+        w_s_dealt = keep.tile([P, PACK, P], U8, name="w_s_dealt", align_bytes=MX_ALIGN)
+        nc.vector.tensor_copy(w_s_dealt[:], w_s[:].rearrange("p (m t) -> p t m", t=PACK))
+        w_first = keep.tile([P, P], U32, name="w_first", align_bytes=MX_ALIGN)
+        w_rest = keep.tile([P, PACK - 1, P], U32, name="w_rest", align_bytes=MX_ALIGN)
         nc.scalar.copy(w_first[:], w_w[:, 0:R:PACK])
         nc.scalar.copy(w_rest[:].rearrange("p t m -> p m t"), w_w[:].rearrange("p (m t) -> p m t", t=PACK)[:, :, 1:PACK])
-        w_t = [w_first[:]] + [w_rest[:, t, :] for t in range(PACK - 1)]
-        xg_w = keep.tile([P, J], U16, name="xg_w", align_bytes=64)
-        xg_s = keep.tile([P, J], U8, name="xg_s", align_bytes=64)
-        a_sb = [keep.tile([P, J], F32, name="a_sb%d" % t, tag="a_sb%d" % t, align_bytes=64) for t in range(PACK)]
+        w_dealt = [w_first[:]] + [w_rest[:, t, :] for t in range(PACK - 1)]
+        xg_w = keep.tile([P, J], U16, name="xg_w", align_bytes=MX_ALIGN)
+        xg_s = keep.tile([P, J], U8, name="xg_s", align_bytes=MX_ALIGN)
+        a_sb = [keep.tile([P, J], F32, name="a_sb%d" % t, tag="a_sb%d" % t, align_bytes=MX_ALIGN) for t in range(PACK)]
 
-        def put_a(t, part, leave_bank, place):
-            bank = product(w_t[t], w_ts[:, t, :], E5M2, xg_w[:, part], xg_s[:, part], E2M1, part.stop - part.start, place)
+        def make_a(t, part, leave_bank, place):
+            width = part.stop - part.start
+            bank = product(w_dealt[t], w_s_dealt[:, t, :], E5M2, xg_w[:, part], xg_s[:, part], E2M1, width, place)
             leave_bank(a_sb[t][:, part], bank)
+
+        def put_a(t, part):
             nc.scalar.activation(pw[t][:].indirect(entries(idx3, part)), a_sb[t][:, part], COPY)
 
         for h in range(2):
             part = slice(h * J // 2, (h + 1) * J // 2)
             nc.vector.tensor_copy(xg_w[:, part], xt_w[:].indirect(entries(idx, part)))
             nc.vector.tensor_copy(xg_s[:, part], xt_s[:].indirect(entries(idx, part)))
-            put_a(0, part, nc.scalar.copy if h == 0 else nc.vector.tensor_copy, 2 * h)
-            put_a(1, part, nc.vector.tensor_copy, 2 * h + 1)
+            make_a(0, part, nc.scalar.copy if h == 0 else nc.vector.tensor_copy, 2 * h)
+            put_a(0, part)
+            make_a(1, part, nc.vector.tensor_copy, 2 * h + 1)
+            put_a(1, part)
+        all_slots = slice(0, J)
         pw.append(zeroed_board(nc.gpsimd, "pw2", "w_w"))
-        put_a(2, slice(0, J), nc.vector.tensor_copy, 4)
-        bank = product(w_t[3], w_ts[:, 3, :], E5M2, xg_w[:], xg_s[:], E2M1, J, 5)
-        nc.vector.tensor_copy(a_sb[3][:], bank)
+        make_a(2, all_slots, nc.vector.tensor_copy, 4)
+        put_a(2, all_slots)
+        make_a(3, all_slots, nc.vector.tensor_copy, 5)
 
-        ws_w = load_words(nc.sync, fp8_rows(ws_words), U32, N, "ws_w", "w_s_rows")
-        wb_w = load_words(nc.sync, fp8_rows(wb_words), U32, N, "wb_w", "w_s")
-        sa_t = keep.tile([P, PACK], F32, name="sa_t", tag="w_first", align_bytes=64)
-        nc.sync.dma_start(sa_t[:], sa.rearrange("(p t) o -> p (t o)", t=PACK))
-        sb_t = keep.tile([P, PACK], F32, name="sb_t", tag="w_ts", align_bytes=64)
-        nc.sync.dma_start(sb_t[:], sb.rearrange("(p t) o -> p (t o)", t=PACK))
-
-        og_w = keep.tile([P, J], U32, name="og_w", align_bytes=64)
-        og_s = keep.tile([P, J], U8, name="og_s", align_bytes=64)
+        og_w = keep.tile([P, J], U32, name="og_w", align_bytes=MX_ALIGN)
+        og_s = keep.tile([P, J], U8, name="og_s", align_bytes=MX_ALIGN)
         nc.vector.tensor_copy(og_w[:], xo_w[:].indirect(idx2[:]))
         nc.vector.tensor_copy(og_s[:], xo_s[:].indirect(idx2[:]))
-        w2_t = keep.tile([P, PACK, P], U32, name="w2_t", align_bytes=64)
-        w2_ts = keep.tile([P, PACK, P], U8, name="w2_ts", align_bytes=64)
+        w2_dealt = keep.tile([P, PACK, P], U32, name="w2_dealt", align_bytes=MX_ALIGN)
+        w2_s_dealt = keep.tile([P, PACK, P], U8, name="w2_s_dealt", align_bytes=MX_ALIGN)
         nc.vector.tensor_copy(
-            w2_t[:].bitcast(I32).rearrange("p t m -> p m t"), w2_w[:].bitcast(I32).rearrange("p (m t) -> p m t", t=PACK)
+            w2_dealt[:].bitcast(I32).rearrange("p t m -> p m t"),
+            w2_w[:].bitcast(I32).rearrange("p (m t) -> p m t", t=PACK),
         )
-        nc.vector.tensor_copy(w2_ts[:], w2_s[:].rearrange("p (m t) -> p t m", t=PACK))
+        nc.vector.tensor_copy(w2_s_dealt[:], w2_s[:].rearrange("p (m t) -> p t m", t=PACK))
         pw.append(zeroed_board(nc.gpsimd, "pw3", "xo_w"))
-        nc.scalar.activation(pw[3][:].indirect(idx3[:]), a_sb[3][:], COPY)
+        put_a(3, all_slots)
+        pv_homes = ("w2_w", "a_sb0")
         pv = []
         b_sb = [keep.tile([P, J], F32, name="b_sb%d" % t) for t in range(PACK)]
         for t in range(PACK):
-            bank = product(w2_t[:, t, :], w2_ts[:, t, :], E4M3, og_w[:], og_s[:], E5M2, J, t)
+            bank = product(w2_dealt[:, t, :], w2_s_dealt[:, t, :], E4M3, og_w[:], og_s[:], E5M2, J, t)
             nc.vector.tensor_copy(b_sb[t][:], bank)
-            if t < 2:
-                pv.append(zeroed_board(nc.gpsimd, "pv%d" % t, ("w2_w", "a_sb0")[t]))
+            if t < len(pv_homes):
+                pv.append(zeroed_board(nc.gpsimd, "pv%d" % t, pv_homes[t]))
 
-        x7_w = keep.tile([P, O], U16, name="x7_w", align_bytes=64)
-        x7_s = keep.tile([P, O], U8, name="x7_s", align_bytes=64)
+        x7_w = keep.tile([P, O], U16, name="x7_w", align_bytes=MX_ALIGN)
+        x7_s = keep.tile([P, O], U8, name="x7_s", align_bytes=MX_ALIGN)
         nc.vector.tensor_copy(x7_w[:], xt_w[:].indirect(idx7[:]))
         nc.vector.tensor_copy(x7_s[:], xt_s[:].indirect(idx7[:]))
         y = [banks.tile([P, O], F32, name="y%d" % u, tag="bank%d" % (2 + u)) for u in range(N // P)]
@@ -170,25 +183,25 @@ def tile_list_ownsum_twotab_further_plain_kernel(
                 rhs=x7_w[:].bitcast(E2M1), rhs_scale=x7_s[:], start=True, stop=False,
             )
 
-        diff = [keep.tile([P, PACK, O // 2], F32, name="diff%d" % h) for h in range(2)]
-        hid = [keep.tile([P, O // 2, PACK], BF16, name="hid%d" % h, align_bytes=64) for h in range(2)]
-        hid_w = keep.tile([P, O], U32, name="hid_w", align_bytes=64)
-        hid_s = keep.tile([P, O], U8, name="hid_s", align_bytes=64)
         halves = [slice(0, O // 2), slice(O // 2, O)]
-        boards = {}
+        diff = [keep.tile([P, PACK, O // 2], F32, name="diff%d" % h) for h in range(2)]
+        hid = [keep.tile([P, O // 2, PACK], BF16, name="hid%d" % h, align_bytes=MX_ALIGN) for h in range(2)]
+        hid_w = keep.tile([P, O], U32, name="hid_w", align_bytes=MX_ALIGN)
+        hid_s = keep.tile([P, O], U8, name="hid_s", align_bytes=MX_ALIGN)
+        pg = []
 
         def put_b(t):
             nc.scalar.activation(pv[t % 2][:].indirect(idx4[:]), b_sb[t][:], COPY)
-            pg = ring.tile([P, C], F32, name="pg")
-            nc.vector.tensor_tensor(pg[:], pw[t][:], pv[t % 2][:], ALU.add)
-            boards[t] = pg
+            summed = ring.tile([P, C], F32, name="summed")
+            nc.vector.tensor_tensor(summed[:], pw[t][:], pv[t % 2][:], ALU.add)
+            pg.append(summed)
 
         def pick(t, parts):
             first = ring.tile([P, O], F32, name="first")
             second = ring.tile([P, O], F32, name="second")
             for part in parts:
-                nc.scalar.activation(first[:, part], boards[t][:].indirect(entries(idx5, part)), COPY, scale=sa_t[:, t : t + 1])
-                nc.scalar.activation(second[:, part], boards[t][:].indirect(entries(idx6, part)), COPY, scale=sb_t[:, t : t + 1])
+                nc.scalar.activation(first[:, part], pg[t][:].indirect(entries(idx5, part)), COPY, scale=sa_t[:, t : t + 1])
+                nc.scalar.activation(second[:, part], pg[t][:].indirect(entries(idx6, part)), COPY, scale=sb_t[:, t : t + 1])
             for h in range(2):
                 nc.vector.tensor_tensor(diff[h][:, t, :], first[:, halves[h]], second[:, halves[h]], ALU.subtract)
             if t % 2 == 1:
@@ -203,17 +216,17 @@ def tile_list_ownsum_twotab_further_plain_kernel(
         pick(PACK - 1, halves)
 
         for h in range(2):
-            nc.vector.quantize_mx(hid_w[:, halves[h]].bitcast(E5M2), hid_s[:, halves[h]], hid[h][:].rearrange("p o t -> p (o t)"))
+            nc.vector.quantize_mx(
+                hid_w[:, halves[h]].bitcast(E5M2), hid_s[:, halves[h]], hid[h][:].rearrange("p o t -> p (o t)")
+            )
+        ways_out = ((nc.vector.tensor_copy, nc.sync), (nc.scalar.copy, nc.scalar))
         for u in range(N // P):
             cols = slice(u * P, (u + 1) * P)
             nc.tensor.matmul_mx(
                 y[u][:], lhsT=wb_w[:, cols].bitcast(E4M3), lhsT_scale=wb_s[:, cols],
                 rhs=hid_w[:].bitcast(E5M2), rhs_scale=hid_s[:], start=False, stop=True,
             )
+            leave_bank, queue = ways_out[u]
             y_sb = keep.tile([P, O], F32, name="y_sb%d" % u)
-            if u == 0:
-                nc.vector.tensor_copy(y_sb[:], y[u][:])
-                nc.sync.dma_start(out[cols, :], y_sb[:])
-            else:
-                nc.scalar.copy(y_sb[:], y[u][:])
-                nc.scalar.dma_start(out[cols, :], y_sb[:])
+            leave_bank(y_sb[:], y[u][:])
+            queue.dma_start(out[cols, :], y_sb[:])

from contextlib import ExitStack

import concourse.mybir as mybir

F32 = mybir.dt.float32
BF16 = mybir.dt.bfloat16
I32 = mybir.dt.int32
U32 = mybir.dt.uint32
U16 = mybir.dt.uint16
U8 = mybir.dt.uint8
E4M3 = mybir.dt.float8_e4m3fn_x4
E5M2 = mybir.dt.float8_e5m2_x4
E2M1 = mybir.dt.float4_e2m1fn_x4
COPY = mybir.ActivationFunctionType.Copy
ALU = mybir.AluOpType

K, T, J, R, F, Z, C, O, N = 512, 1024, 256, 512, 512, 1024, 512, 128, 256
P = 128
PACK = 4
QUADRANTS = 4
QUADRANT = P // QUADRANTS
SCALE_ROWS = 4
LIST_ROWS = 16
MX_ALIGN = 64
FLOPS = 2 * (K * R * J + F * R * J + R * N * O + K * N * O)


def tile_list_ownsum_twotab_further_plain_kernel(
    tc, xt_words, xt_scales, xo_words, xo_scales, w_words, w_scales, w2_words, w2_scales, sa, sb,
    wb_words, wb_scales, ws_words, ws_scales, offs, offs2, offs3, offs4, offs5, offs6, offs7, out,
):
    nc = tc.nc
    with ExitStack() as ctx:
        lists = ctx.enter_context(tc.tile_pool(name="lists", bufs=1))
        keep = ctx.enter_context(tc.tile_pool(name="keep", bufs=1))
        ring = ctx.enter_context(tc.tile_pool(name="ring", bufs=2))
        banks = ctx.enter_context(tc.psum_pool(name="banks", bufs=1))

        def load_list(source, name):
            held = lists.tile(list(source.shape), U16, name=name)
            nc.sync.dma_start(held[:], source)
            return held

        def entries(held, part):
            return held[:, part.start // LIST_ROWS : part.stop // LIST_ROWS]

        def load_words(source, dtype, columns, name):
            held = keep.tile([P, columns], dtype, name=name, tag=name, align_bytes=MX_ALIGN)
            nc.sync.dma_start(held[:].bitcast(I32), source.bitcast(I32))
            return held

        def fp8_rows(words):
            return words[0].rearrange("p n t -> p (n t)")

        def zeroed_scales(columns, name):
            held = keep.tile([P, columns], U8, name=name, align_bytes=MX_ALIGN)
            nc.vector.memset(held[:].bitcast(I32), 0)
            return held

        def live_rows(held, q):
            return held[QUADRANT * q : QUADRANT * q + SCALE_ROWS, :].bitcast(I32)

        def load_scales(held, source):
            for q in range(QUADRANTS):
                rows = source[0, SCALE_ROWS * q : SCALE_ROWS * (q + 1), :]
                nc.sync.dma_start(live_rows(held, q), rows.bitcast(I32))

        def load_row_weights(source, name):
            held = keep.tile([P, PACK], F32, name=name)
            nc.sync.dma_start(held[:], source.rearrange("(p t) o -> p (t o)", t=PACK))
            return held

        def zeroed_board(engine, name, tag):
            held = keep.tile([P, C], F32, name=name, tag=tag, align_bytes=MX_ALIGN)
            engine.memset(held[:], 0.0)
            return held

        def product(weights, weight_scales, weight_format, moving, moving_scales, moving_format, width, place):
            bank = banks.tile([P, J], F32, name="bank", tag="bank%d" % place)
            nc.tensor.matmul_mx(
                bank[:, 0:width], lhsT=weights.bitcast(weight_format), lhsT_scale=weight_scales,
                rhs=moving.bitcast(moving_format), rhs_scale=moving_scales, start=True, stop=True,
            )
            return bank[:, 0:width]

        xt_s = zeroed_scales(T, "xt_s")
        w_s = zeroed_scales(R, "w_s")
        xo_s = zeroed_scales(Z, "xo_s")
        w2_s = zeroed_scales(R, "w2_s")
        idx = load_list(offs, "idx")
        w_s_rows = keep.tile([SCALE_ROWS, QUADRANTS, R // 4], I32, name="w_s_rows")
        nc.sync.dma_start(w_s_rows[:], w_scales[0].bitcast(I32).rearrange("(q i) n -> i q n", i=SCALE_ROWS))
        xt_w = load_words(xt_words[0], U16, T, "xt_w")
        load_scales(xt_s, xt_scales)
        w_w = load_words(fp8_rows(w_words), U32, R, "w_w")
        idx3 = load_list(offs3, "idx3")
        pw = [zeroed_board(nc.vector, "pw%d" % t, "pw%d" % t) for t in range(2)]

        ws_s = zeroed_scales(N, "ws_s")
        wb_s = zeroed_scales(N, "wb_s")
        idx2 = load_list(offs2, "idx2")
        load_scales(xo_s, xo_scales)
        xo_w = load_words(fp8_rows(xo_words), U32, Z, "xo_w")
        w2_w = load_words(fp8_rows(w2_words), U32, R, "w2_w")
        load_scales(w2_s, w2_scales)
        idx4 = load_list(offs4, "idx4")
        idx7 = load_list(offs7, "idx7")
        idx5 = load_list(offs5, "idx5")
        idx6 = load_list(offs6, "idx6")
        sa_t = load_row_weights(sa, "sa_t")
        sb_t = load_row_weights(sb, "sb_t")
        ws_w = load_words(fp8_rows(ws_words), U32, N, "ws_w")
        load_scales(ws_s, ws_scales)
        wb_w = load_words(fp8_rows(wb_words), U32, N, "wb_w")
        load_scales(wb_s, wb_scales)

        for q in range(QUADRANTS):
            nc.vector.tensor_copy(live_rows(w_s, q), w_s_rows[:, q, :])
        w_s_dealt = keep.tile([P, PACK, P], U8, name="w_s_dealt", align_bytes=MX_ALIGN)
        nc.vector.tensor_copy(w_s_dealt[:], w_s[:].rearrange("p (m t) -> p t m", t=PACK))
        w_first = keep.tile([P, P], U32, name="w_first", align_bytes=MX_ALIGN)
        w_rest = keep.tile([P, PACK - 1, P], U32, name="w_rest", align_bytes=MX_ALIGN)
        nc.scalar.copy(w_first[:], w_w[:, 0:R:PACK])
        nc.scalar.copy(w_rest[:].rearrange("p t m -> p m t"), w_w[:].rearrange("p (m t) -> p m t", t=PACK)[:, :, 1:PACK])
        w_dealt = [w_first[:]] + [w_rest[:, t, :] for t in range(PACK - 1)]
        xg_w = keep.tile([P, J], U16, name="xg_w", align_bytes=MX_ALIGN)
        xg_s = keep.tile([P, J], U8, name="xg_s", align_bytes=MX_ALIGN)
        a_sb = [keep.tile([P, J], F32, name="a_sb%d" % t, tag="a_sb%d" % t, align_bytes=MX_ALIGN) for t in range(PACK)]

        def make_a(t, part, leave_bank, place):
            width = part.stop - part.start
            bank = product(w_dealt[t], w_s_dealt[:, t, :], E5M2, xg_w[:, part], xg_s[:, part], E2M1, width, place)
            leave_bank(a_sb[t][:, part], bank)

        def put_a(t, part):
            nc.scalar.activation(pw[t][:].indirect(entries(idx3, part)), a_sb[t][:, part], COPY)

        for h in range(2):
            part = slice(h * J // 2, (h + 1) * J // 2)
            nc.vector.tensor_copy(xg_w[:, part], xt_w[:].indirect(entries(idx, part)))
            nc.vector.tensor_copy(xg_s[:, part], xt_s[:].indirect(entries(idx, part)))
            make_a(0, part, nc.scalar.copy if h == 0 else nc.vector.tensor_copy, 2 * h)
            put_a(0, part)
            make_a(1, part, nc.vector.tensor_copy, 2 * h + 1)
            put_a(1, part)
        all_slots = slice(0, J)
        pw.append(zeroed_board(nc.gpsimd, "pw2", "w_w"))
        make_a(2, all_slots, nc.vector.tensor_copy, 4)
        put_a(2, all_slots)
        make_a(3, all_slots, nc.vector.tensor_copy, 5)

        og_w = keep.tile([P, J], U32, name="og_w", align_bytes=MX_ALIGN)
        og_s = keep.tile([P, J], U8, name="og_s", align_bytes=MX_ALIGN)
        nc.vector.tensor_copy(og_w[:], xo_w[:].indirect(idx2[:]))
        nc.vector.tensor_copy(og_s[:], xo_s[:].indirect(idx2[:]))
        w2_dealt = keep.tile([P, PACK, P], U32, name="w2_dealt", align_bytes=MX_ALIGN)
        w2_s_dealt = keep.tile([P, PACK, P], U8, name="w2_s_dealt", align_bytes=MX_ALIGN)
        nc.vector.tensor_copy(
            w2_dealt[:].bitcast(I32).rearrange("p t m -> p m t"),
            w2_w[:].bitcast(I32).rearrange("p (m t) -> p m t", t=PACK),
        )
        nc.vector.tensor_copy(w2_s_dealt[:], w2_s[:].rearrange("p (m t) -> p t m", t=PACK))
        pw.append(zeroed_board(nc.gpsimd, "pw3", "xo_w"))
        put_a(3, all_slots)
        pv_homes = ("w2_w", "a_sb0")
        pv = []
        b_sb = [keep.tile([P, J], F32, name="b_sb%d" % t) for t in range(PACK)]
        for t in range(PACK):
            bank = product(w2_dealt[:, t, :], w2_s_dealt[:, t, :], E4M3, og_w[:], og_s[:], E5M2, J, t)
            nc.vector.tensor_copy(b_sb[t][:], bank)
            if t < len(pv_homes):
                pv.append(zeroed_board(nc.gpsimd, "pv%d" % t, pv_homes[t]))

        x7_w = keep.tile([P, O], U16, name="x7_w", align_bytes=MX_ALIGN)
        x7_s = keep.tile([P, O], U8, name="x7_s", align_bytes=MX_ALIGN)
        nc.vector.tensor_copy(x7_w[:], xt_w[:].indirect(idx7[:]))
        nc.vector.tensor_copy(x7_s[:], xt_s[:].indirect(idx7[:]))
        y = [banks.tile([P, O], F32, name="y%d" % u, tag="bank%d" % (2 + u)) for u in range(N // P)]
        for u in range(N // P):
            cols = slice(u * P, (u + 1) * P)
            nc.tensor.matmul_mx(
                y[u][:], lhsT=ws_w[:, cols].bitcast(E4M3), lhsT_scale=ws_s[:, cols],
                rhs=x7_w[:].bitcast(E2M1), rhs_scale=x7_s[:], start=True, stop=False,
            )

        halves = [slice(0, O // 2), slice(O // 2, O)]
        diff = [keep.tile([P, PACK, O // 2], F32, name="diff%d" % h) for h in range(2)]
        hid = [keep.tile([P, O // 2, PACK], BF16, name="hid%d" % h, align_bytes=MX_ALIGN) for h in range(2)]
        hid_w = keep.tile([P, O], U32, name="hid_w", align_bytes=MX_ALIGN)
        hid_s = keep.tile([P, O], U8, name="hid_s", align_bytes=MX_ALIGN)
        pg = []

        def put_b(t):
            nc.scalar.activation(pv[t % 2][:].indirect(idx4[:]), b_sb[t][:], COPY)
            summed = ring.tile([P, C], F32, name="summed")
            nc.vector.tensor_tensor(summed[:], pw[t][:], pv[t % 2][:], ALU.add)
            pg.append(summed)

        def pick(t, parts):
            first = ring.tile([P, O], F32, name="first")
            second = ring.tile([P, O], F32, name="second")
            for part in parts:
                nc.scalar.activation(first[:, part], pg[t][:].indirect(entries(idx5, part)), COPY, scale=sa_t[:, t : t + 1])
                nc.scalar.activation(second[:, part], pg[t][:].indirect(entries(idx6, part)), COPY, scale=sb_t[:, t : t + 1])
            for h in range(2):
                nc.vector.tensor_tensor(diff[h][:, t, :], first[:, halves[h]], second[:, halves[h]], ALU.subtract)
            if t % 2 == 1:
                for h in range(2):
                    pair = diff[h][:, t - 1 : t + 1, :].rearrange("p t o -> p o t")
                    nc.vector.scalar_tensor_tensor(hid[h][:, :, t - 1 : t + 1], pair, -1.0, pair, ALU.mult, ALU.max)

        put_b(0)
        for t in range(1, PACK):
            put_b(t)
            pick(t - 1, [slice(0, O)])
        pick(PACK - 1, halves)

        for h in range(2):
            nc.vector.quantize_mx(
                hid_w[:, halves[h]].bitcast(E5M2), hid_s[:, halves[h]], hid[h][:].rearrange("p o t -> p (o t)")
            )
        ways_out = ((nc.vector.tensor_copy, nc.sync), (nc.scalar.copy, nc.scalar))
        for u in range(N // P):
            cols = slice(u * P, (u + 1) * P)
            nc.tensor.matmul_mx(
                y[u][:], lhsT=wb_w[:, cols].bitcast(E4M3), lhsT_scale=wb_s[:, cols],
                rhs=hid_w[:].bitcast(E5M2), rhs_scale=hid_s[:], start=False, stop=True,
            )
            leave_bank, queue = ways_out[u]
            y_sb = keep.tile([P, O], F32, name="y_sb%d" % u)
            leave_bank(y_sb[:], y[u][:])
            queue.dma_start(out[cols, :], y_sb[:])
